import numpy as np
import ml_dtypes


def mxq(x, axis, fmt="e4m3"):
    dtype, down = {"e4m3": (ml_dtypes.float8_e4m3fn, 7), "e5m2": (ml_dtypes.float8_e5m2, 14)}[fmt]
    v = np.moveaxis(np.asarray(x, np.float32).astype(ml_dtypes.bfloat16).astype(np.float64), axis, -1)
    blocks = v.reshape(v.shape[:-1] + (-1, 32))
    amax = np.abs(blocks).max(-1, keepdims=True)
    byte = np.maximum(np.where(amax > 0, np.frexp(amax)[1] - 1 + 127, 0) - down, 1)
    scale = np.exp2(byte - 127.0)
    codes = (blocks / scale).astype(np.float32).astype(dtype).astype(np.float64)
    return np.moveaxis((codes * scale).reshape(v.shape), -1, axis)


WIDE = False


def mx_kscale(k):
    if not WIDE:
        return np.ones(k)
    levels = np.array([30, -30])
    if k % 512:
        return np.exp2(np.random.permutation(np.resize(levels, k // 32))).repeat(32)
    a = np.empty((k // 512, 16))
    for p in range(k // 512):
        a[p, :8] = np.random.permutation(np.resize(levels, 8))
        for g in range(8):
            far = levels[np.abs(levels - a[p, g]) >= 10]
            a[p, g + 8] = far[np.random.randint(len(far))]
    return np.exp2(a.ravel()).repeat(32)


def f64(x):
    return np.asarray(x).astype(np.float64)


def striped(idx):
    return np.tile(np.asarray(idx).reshape(-1, 16).T, (8, 1)).astype(np.uint16)


def unstriped(offs):
    return offs[:16].T.reshape(-1).astype(np.int64)


K, J, N, T, V, C, E = 256, 1024, 256, 2048, 2048, 128, 128


def setup_inputs():
    n = np.random.standard_normal
    idx = np.random.permutation(T)[:J]
    idx2 = np.random.permutation(T)[:J]
    idx3 = np.random.permutation(V)[:J]
    idx4 = np.random.permutation(N)[:E]
    fj = mx_kscale(J)
    return {
        "xf": (n((K, T))).astype(np.float32),
        "ra": (np.random.uniform(0.5, 1.5, (1, J)) * fj).astype(np.float32),
        "gt": (n((N, V)) * np.exp(0.5 * n((1, V)))).astype(np.float32),
        "rb": (np.random.uniform(0.5, 1.5, (1, J)) / fj).astype(np.float32),
        "old": (0.5 * n((K, E))).astype(np.float32),
        "offs": striped(idx),
        "offs2": striped(idx2),
        "offs3": striped(idx3),
        "offs4": striped(idx4),
    }


def reference(xf, ra, gt, rb, old, offs, offs2, offs3, offs4):
    idx = unstriped(offs)
    idx2 = unstriped(offs2)
    idx3 = unstriped(offs3)
    idx4 = unstriped(offs4)
    us = (f64(xf)[:, idx] - f64(xf)[:, idx2]) * f64(ra)
    uj = us.T
    gg = f64(gt)[:, idx3]
    c1 = gg.reshape(N, C, J // C).mean(axis=2)
    c2 = np.repeat(c1, J // C, axis=1)
    gs = (gg - c2) * f64(rb)
    gj = gs.T
    ujq = mxq(uj, 0, "e5m2")
    gjq = mxq(gj, 0, "e5m2")
    w = ujq.T @ gjq
    y = 0.04 * w[:, idx4] + f64(old)
    return y

@@ -1,0 +1,170 @@
+from contextlib import ExitStack
+
+import concourse.mybir as mybir
+from concourse.masks import make_identity
+
+K, J, N, T, E = 256, 1024, 256, 2048, 128
+FLOPS = 2 * K * J * N
+
+F32 = mybir.dt.float32
+BF16 = mybir.dt.bfloat16
+U32 = mybir.dt.uint32
+U16 = mybir.dt.uint16
+U8 = mybir.dt.uint8
+E5M2X4 = mybir.dt.float8_e5m2_x4
+ALU = mybir.AluOpType
+COPY = mybir.ActivationFunctionType.Copy
+
+P = 128
+PACK = 4
+PASS = P * PACK
+PASSES = J // PASS
+SET = 8
+LIST_COLS = PASS // 16
+
+
+def tile_list_moment_gaps_centred_columns_kernel(tc, xf, ra, gt, rb, old, offs, offs2, offs3, offs4, out):
+    nc = tc.nc
+    with ExitStack() as ctx:
+        lists = ctx.enter_context(tc.tile_pool(name="lists", bufs=1))
+        keep = ctx.enter_context(tc.tile_pool(name="keep", bufs=1))
+        turn = ctx.enter_context(tc.psum_pool(name="turn", bufs=6))
+        sums = ctx.enter_context(tc.psum_pool(name="sums", bufs=1))
+
+        first = lists.tile([P, J // 16], U16, name="first")
+        second = lists.tile([P, J // 16], U16, name="second")
+        third = lists.tile([P, J // 16], U16, name="third")
+        fourth = lists.tile([P, E // 16], U16, name="fourth")
+        x_rows = [keep.tile([P, T], F32, name="x_rows%d" % i) for i in range(2)]
+        g_rows = [keep.tile([P, T], F32, name="g_rows%d" % i) for i in range(2)]
+        ra_t = keep.tile([P, PASSES, 8], F32, name="ra_t")
+        rb_t = keep.tile([P, PASSES, 8], F32, name="rb_t")
+        old_t = keep.tile([P, 2, E], F32, name="old_t")
+        ident = keep.tile([P, P], F32, name="ident")
+
+        nc.sync.dma_start(x_rows[0][:], xf[0:P, :])
+        nc.sync.dma_start(second[:], offs2)
+        nc.sync.dma_start(first[:], offs)
+        nc.sync.dma_start(g_rows[0][:], gt[0:P, :])
+        nc.sync.dma_start(third[:], offs3)
+        nc.sync.dma_start(ra_t[:, :, 0:PACK], ra.rearrange("o (a p t) -> p (o a) t", p=P, t=PACK))
+        nc.sync.dma_start(g_rows[1][:], gt[P : 2 * P, :])
+        nc.sync.dma_start(rb_t[:, :, 0:PACK], rb.rearrange("o (a p t) -> p (o a) t", p=P, t=PACK))
+        nc.sync.dma_start(x_rows[1][:], xf[P : 2 * P, :])
+        nc.sync.dma_start(fourth[:], offs4)
+        nc.sync.dma_start(old_t[:], old.rearrange("(i p) e -> p i e", p=P))
+        make_identity(nc, ident[:])
+
+        def entries(lst, a):
+            return lst[:, a * LIST_COLS : (a + 1) * LIST_COLS]
+
+        u_bf = [keep.tile([P, PASSES, P, PACK], BF16, name="u_bf%d" % i, align_bytes=64) for i in range(2)]
+        u_codes = [keep.tile([P, PASSES, P], U32, name="u_codes%d" % i, align_bytes=64) for i in range(2)]
+        u_scales = [keep.tile([P, PASSES, P], U8, name="u_scales%d" % i, align_bytes=64) for i in range(2)]
+        g_bf = [keep.tile([P, 2, P, PACK], BF16, name="g_bf%d" % a, align_bytes=64) for a in range(PASSES)]
+        g_codes = [keep.tile([P, N], U32, name="g_codes%d" % a, align_bytes=64) for a in range(PASSES)]
+        g_scales = [keep.tile([P, N], U8, name="g_scales%d" % a, align_bytes=64) for a in range(PASSES)]
+        gaps, picked, means, banks = {}, {}, {}, {}
+
+        def gather_x(i, a):
+            sub = keep.tile([P, PASS], F32, name="sub%d%d" % (i, a))
+            nc.scalar.activation(sub[:], x_rows[i][:].indirect(entries(second, a)), COPY)
+            gaps[i, a] = keep.tile([P, PASS], F32, name="gap%d%d" % (i, a))
+            nc.vector.tensor_tensor(gaps[i, a][:], x_rows[i][:].indirect(entries(first, a)), sub[:], ALU.subtract)
+
+        def gather_g(i, a):
+            picked[i, a] = keep.tile([P, PASS], F32, name="picked%d%d" % (i, a))
+            nc.scalar.activation(picked[i, a][:], g_rows[i][:].indirect(entries(third, a)), COPY)
+
+        def mean_g(i, a):
+            sets = PASS // SET
+            total = keep.tile([P, sets], F32, name="total%d%d" % (i, a))
+            nc.vector.tensor_reduce(
+                total[:], picked[i, a][:].rearrange("p (c s) -> p c s", s=SET), mybir.AxisListType.X, ALU.add
+            )
+            means[i, a] = keep.tile([P, sets, 2], F32, name="mean%d%d" % (i, a))
+            nc.gpsimd.tensor_scalar(
+                means[i, a][:], total[:].unsqueeze(2).to_broadcast([P, sets, 2]), -1.0 / SET, 0.0, ALU.mult, ALU.add
+            )
+
+        def turn_x(i, a):
+            bank = turn.tile([P, PACK, P], F32, name="bank")
+            banks["x", i, a] = bank
+            for t in range(PACK):
+                nc.tensor.matmul(bank[:, t, :], gaps[i, a][:, t::PACK], ident[:], start=(t == 0), stop=(t == PACK - 1), is_transpose=True)
+
+        def turn_g(i, a):
+            bank = turn.tile([P, PACK, P], F32, name="bank")
+            banks["g", i, a] = bank
+            for t in range(PACK):
+                nc.tensor.matmul(bank[:, t, :], picked[i, a][:, t::PACK], ident[:], start=(t == 0), stop=False, is_transpose=True)
+            for t in range(PACK):
+                nc.tensor.matmul(
+                    bank[:, t, :], means[i, a][:].rearrange("p c e -> p (c e)"), ident[:], start=False, stop=(t == PACK - 1), is_transpose=True
+                )
+
+        def weigh(dst, bank, weights, a):
+            nc.vector.tensor_tensor(
+                dst, bank[:].rearrange("p t c -> p c t"), weights[:, a : a + 1, 0:PACK].to_broadcast([P, P, PACK]), ALU.mult
+            )
+
+        def quantize_x(i, a):
+            nc.vector.quantize_mx(
+                out=u_codes[i][:, a, :].bitcast(E5M2X4), scales=u_scales[i][:, a, :], in_=u_bf[i][:, a].rearrange("p c t -> p (c t)")
+            )
+
+        def quantize_g(a):
+            nc.vector.quantize_mx(
+                out=g_codes[a][:].bitcast(E5M2X4), scales=g_scales[a][:], in_=g_bf[a][:].rearrange("p i c t -> p (i c t)")
+            )
+
+        moments = [sums.tile([P, N], F32, name="moment%d" % i) for i in range(2)]
+
+        def multiply(i, a):
+            nc.tensor.matmul_mx(
+                out=moments[i][:],
+                lhsT=u_codes[i][:, a, :].bitcast(E5M2X4),
+                lhsT_scale=u_scales[i][:, a, :],
+                rhs=g_codes[a][:].bitcast(E5M2X4),
+                rhs_scale=g_scales[a][:],
+                start=(a == 0),
+                stop=(a == PASSES - 1),
+            )
+
+        def finish(i):
+            w = keep.tile([P, N], F32, name="w%d" % i)
+            nc.scalar.copy(w[:], moments[i][:])
+            cols = keep.tile([P, E], F32, name="cols%d" % i)
+            nc.vector.tensor_copy(cols[:], w[:].indirect(fourth[:]))
+            y = keep.tile([P, E], F32, name="y%d" % i)
+            nc.vector.scalar_tensor_tensor(y[:], cols[:], 0.04, old_t[:, i, :], ALU.mult, ALU.add)
+            nc.sync.dma_start(out[i * P : (i + 1) * P, :], y[:])
+
+        for a in range(PASSES):
+            gather_x(0, a)
+            turn_x(0, a)
+        for i in range(2):
+            for a in range(PASSES):
+                gather_g(i, a)
+                if i == 0:
+                    weigh(u_bf[0][:, a], banks["x", 0, a], ra_t, a)
+                mean_g(i, a)
+                if i == 1:
+                    weigh(g_bf[a][:, 0], banks["g", 0, a], rb_t, a)
+                    quantize_x(0, a)
+                turn_g(i, a)
+        for a in range(PASSES):
+            weigh(g_bf[a][:, 1], banks["g", 1, a], rb_t, a)
+            gather_x(1, a)
+            turn_x(1, a)
+            quantize_g(a)
+        for a in range(PASSES):
+            multiply(0, a)
+        weigh(u_bf[1][:, 0], banks["x", 1, 0], ra_t, 0)
+        finish(0)
+        quantize_x(1, 0)
+        weigh(u_bf[1][:, 1], banks["x", 1, 1], ra_t, 1)
+        multiply(1, 0)
+        quantize_x(1, 1)
+        multiply(1, 1)
+        finish(1)

@@ -28,7 +28,7 @@ def tile_list_moment_gaps_centred_columns_kernel(tc, xf, ra, gt, rb, old, offs, 
     with ExitStack() as ctx:
         lists = ctx.enter_context(tc.tile_pool(name="lists", bufs=1))
         keep = ctx.enter_context(tc.tile_pool(name="keep", bufs=1))
-        turn = ctx.enter_context(tc.psum_pool(name="turn", bufs=6))
+        turn = ctx.enter_context(tc.psum_pool(name="turn", bufs=4))
         sums = ctx.enter_context(tc.psum_pool(name="sums", bufs=1))
 
         first = lists.tile([P, J // 16], U16, name="first")
@@ -45,32 +45,67 @@ def tile_list_moment_gaps_centred_columns_kernel(tc, xf, ra, gt, rb, old, offs, 
         nc.sync.dma_start(x_rows[0][:], xf[0:P, :])
         nc.sync.dma_start(second[:], offs2)
         nc.sync.dma_start(first[:], offs)
+        nc.sync.dma_start(ra_t[:, :, 0:PACK], ra.rearrange("o (a p t) -> p (o a) t", p=P, t=PACK))
         nc.sync.dma_start(g_rows[0][:], gt[0:P, :])
         nc.sync.dma_start(third[:], offs3)
-        nc.sync.dma_start(ra_t[:, :, 0:PACK], ra.rearrange("o (a p t) -> p (o a) t", p=P, t=PACK))
-        nc.sync.dma_start(g_rows[1][:], gt[P : 2 * P, :])
         nc.sync.dma_start(rb_t[:, :, 0:PACK], rb.rearrange("o (a p t) -> p (o a) t", p=P, t=PACK))
+        nc.sync.dma_start(g_rows[1][:], gt[P : 2 * P, :])
         nc.sync.dma_start(x_rows[1][:], xf[P : 2 * P, :])
         nc.sync.dma_start(fourth[:], offs4)
         nc.sync.dma_start(old_t[:], old.rearrange("(i p) e -> p i e", p=P))
+        warm = keep.tile([P, 8], F32, name="warm")
+        nc.vector.memset(warm[:], 0.0)
+        nc.scalar.activation(warm[:, 0:1], warm[:, 4:5], COPY)
         make_identity(nc, ident[:])
 
-        def entries(lst, a):
-            return lst[:, a * LIST_COLS : (a + 1) * LIST_COLS]
+        def entries(lst, a, start=0, stop=PASS):
+            return lst[:, a * LIST_COLS + start // 16 : a * LIST_COLS + stop // 16]
+
+        ra_rows = [sums.tile([P, PACK, P], F32, name="ra_rows%d" % a) for a in range(PASSES)]
+        for a in range(PASSES):
+            for t in range(PACK):
+                nc.tensor.transpose(ra_rows[a][:, t, :], ra_t[:, a, t : t + 1].to_broadcast([P, P]), ident[:])
 
         u_bf = [keep.tile([P, PASSES, P, PACK], BF16, name="u_bf%d" % i, align_bytes=64) for i in range(2)]
         u_codes = [keep.tile([P, PASSES, P], U32, name="u_codes%d" % i, align_bytes=64) for i in range(2)]
         u_scales = [keep.tile([P, PASSES, P], U8, name="u_scales%d" % i, align_bytes=64) for i in range(2)]
-        g_bf = [keep.tile([P, 2, P, PACK], BF16, name="g_bf%d" % a, align_bytes=64) for a in range(PASSES)]
+        g_bf = [keep.tile([P, PASSES, P, PACK], BF16, name="g_bf0", align_bytes=64)]
         g_codes = [keep.tile([P, N], U32, name="g_codes%d" % a, align_bytes=64) for a in range(PASSES)]
         g_scales = [keep.tile([P, N], U8, name="g_scales%d" % a, align_bytes=64) for a in range(PASSES)]
         gaps, picked, means, banks = {}, {}, {}, {}
 
-        def gather_x(i, a):
-            sub = keep.tile([P, PASS], F32, name="sub%d%d" % (i, a))
-            nc.scalar.activation(sub[:], x_rows[i][:].indirect(entries(second, a)), COPY)
+        def gather_x(i, a, cuts, fused):
             gaps[i, a] = keep.tile([P, PASS], F32, name="gap%d%d" % (i, a))
-            nc.vector.tensor_tensor(gaps[i, a][:], x_rows[i][:].indirect(entries(first, a)), sub[:], ALU.subtract)
+            for q, (start, stop) in enumerate(zip(cuts[:-1], cuts[1:])):
+                two = keep.tile([P, stop - start], F32, name="two%d%d%d" % (i, a, q), align_bytes=64)
+                nc.scalar.activation(two[:], x_rows[i][:].indirect(entries(second, a, start, stop)), COPY)
+                if fused:
+                    nc.vector.tensor_tensor(
+                        gaps[i, a][:, start:stop], x_rows[i][:].indirect(entries(first, a, start, stop)), two[:], ALU.subtract
+                    )
+                else:
+                    one = keep.tile([P, stop - start], F32, name="one%d%d%d" % (i, a, q))
+                    nc.scalar.activation(one[:], x_rows[i][:].indirect(entries(first, a, start, stop)), COPY)
+                    nc.gpsimd.tensor_tensor(gaps[i, a][:, start:stop], one[:], two[:], ALU.subtract)
+
+        def weigh_x(i, a, cuts):
+            rounded = keep.tile([P, P, PACK], BF16, name="rounded%d%d" % (i, a))
+            for start, stop in zip(cuts[:-1], cuts[1:]):
+                ps = slice(start // PACK, stop // PACK)
+                nc.vector.tensor_tensor(
+                    rounded[:, ps, :],
+                    ra_rows[a][:, :, ps].rearrange("k t p -> k p t"),
+                    gaps[i, a][:, start:stop].rearrange("k (p t) -> k p t", t=PACK),
+                    ALU.mult,
+                )
+            words = rounded[:].rearrange("k p t -> k (p t)").bitcast(F32)
+            bank = turn.tile([P, 2, P], F32, name="bank")
+            for u in range(2):
+                nc.tensor.transpose(bank[:, u, :], words[:, u::2], ident[:])
+            nc.scalar.copy(
+                u_bf[i][:, a].rearrange("p c t -> p (c t)").bitcast(F32).rearrange("p (c u) -> p c u", u=2),
+                bank[:].rearrange("p u c -> p c u"),
+            )
 
         def gather_g(i, a):
             picked[i, a] = keep.tile([P, PASS], F32, name="picked%d%d" % (i, a))
@@ -91,7 +126,7 @@ def tile_list_moment_gaps_centred_columns_kernel(tc, xf, ra, gt, rb, old, offs, 
             bank = turn.tile([P, PACK, P], F32, name="bank")
             banks["x", i, a] = bank
             for t in range(PACK):
-                nc.tensor.matmul(bank[:, t, :], gaps[i, a][:, t::PACK], ident[:], start=(t == 0), stop=(t == PACK - 1), is_transpose=True)
+                nc.tensor.transpose(bank[:, t, :], gaps[i, a][:, t::PACK], ident[:])
 
         def turn_g(i, a):
             bank = turn.tile([P, PACK, P], F32, name="bank")
@@ -108,14 +143,17 @@ def tile_list_moment_gaps_centred_columns_kernel(tc, xf, ra, gt, rb, old, offs, 
                 dst, bank[:].rearrange("p t c -> p c t"), weights[:, a : a + 1, 0:PACK].to_broadcast([P, P, PACK]), ALU.mult
             )
 
-        def quantize_x(i, a):
+        def quantize_x(i, a0, a1):
             nc.vector.quantize_mx(
-                out=u_codes[i][:, a, :].bitcast(E5M2X4), scales=u_scales[i][:, a, :], in_=u_bf[i][:, a].rearrange("p c t -> p (c t)")
+                out=u_codes[i][:, a0:a1, :].rearrange("p a c -> p (a c)").bitcast(E5M2X4),
+                scales=u_scales[i][:, a0:a1, :].rearrange("p a c -> p (a c)"),
+                in_=u_bf[i][:, a0:a1].rearrange("p a c t -> p (a c t)"),
             )
 
-        def quantize_g(a):
+        def quantize_g(i, a):
+            cols = slice(i * P, (i + 1) * P)
             nc.vector.quantize_mx(
-                out=g_codes[a][:].bitcast(E5M2X4), scales=g_scales[a][:], in_=g_bf[a][:].rearrange("p i c t -> p (i c t)")
+                out=g_codes[a][:, cols].bitcast(E5M2X4), scales=g_scales[a][:, cols], in_=g_bf[i][:, a].rearrange("p c t -> p (c t)")
             )
 
         moments = [sums.tile([P, N], F32, name="moment%d" % i) for i in range(2)]
@@ -141,30 +179,35 @@ def tile_list_moment_gaps_centred_columns_kernel(tc, xf, ra, gt, rb, old, offs, 
             nc.sync.dma_start(out[i * P : (i + 1) * P, :], y[:])
 
         for a in range(PASSES):
-            gather_x(0, a)
+            gather_x(0, a, (0, 256, 512), True)
             turn_x(0, a)
-        for i in range(2):
-            for a in range(PASSES):
-                gather_g(i, a)
-                if i == 0:
-                    weigh(u_bf[0][:, a], banks["x", 0, a], ra_t, a)
-                mean_g(i, a)
-                if i == 1:
-                    weigh(g_bf[a][:, 0], banks["g", 0, a], rb_t, a)
-                    quantize_x(0, a)
-                turn_g(i, a)
         for a in range(PASSES):
-            weigh(g_bf[a][:, 1], banks["g", 1, a], rb_t, a)
-            gather_x(1, a)
-            turn_x(1, a)
-            quantize_g(a)
+            gather_g(0, a)
+            weigh(u_bf[0][:, a], banks["x", 0, a], ra_t, a)
+            mean_g(0, a)
+            turn_g(0, a)
+        quantize_x(0, 0, 2)
+        for a in range(PASSES):
+            gather_g(1, a)
+            mean_g(1, a)
+            weigh(g_bf[0][:, a], banks["g", 0, a], rb_t, a)
+            turn_g(1, a)
+        gather_x(1, 0, (0, 512), True)
+        gather_x(1, 1, (0, 384, 512), False)
+        g_bf.append(keep.tile([P, PASSES, P, PACK], BF16, name="two100", align_bytes=64))
+        quantize_g(0, 0)
+        quantize_g(0, 1)
+        weigh(g_bf[1][:, 0], banks["g", 1, 0], rb_t, 0)
+        weigh_x(1, 0, (0, 512))
+        quantize_g(1, 0)
+        weigh(g_bf[1][:, 1], banks["g", 1, 1], rb_t, 1)
+        weigh_x(1, 1, (0, 384, 512))
+        quantize_g(1, 1)
         for a in range(PASSES):
             multiply(0, a)
-        weigh(u_bf[1][:, 0], banks["x", 1, 0], ra_t, 0)
-        finish(0)
-        quantize_x(1, 0)
-        weigh(u_bf[1][:, 1], banks["x", 1, 1], ra_t, 1)
+        quantize_x(1, 0, 1)
         multiply(1, 0)
-        quantize_x(1, 1)
+        quantize_x(1, 1, 2)
         multiply(1, 1)
+        finish(0)
         finish(1)

@@ -69,13 +69,12 @@ def tile_list_moment_gaps_centred_columns_kernel(tc, xf, ra, gt, rb, old, offs, 
         u_bf = [keep.tile([P, PASSES, P, PACK], BF16, name="u_bf%d" % i, align_bytes=64) for i in range(2)]
         u_codes = [keep.tile([P, PASSES, P], U32, name="u_codes%d" % i, align_bytes=64) for i in range(2)]
         u_scales = [keep.tile([P, PASSES, P], U8, name="u_scales%d" % i, align_bytes=64) for i in range(2)]
-        g_bf = [keep.tile([P, PASSES, P, PACK], BF16, name="g_bf0", align_bytes=64)]
-        g_codes = [keep.tile([P, N], U32, name="g_codes%d" % a, align_bytes=64) for a in range(PASSES)]
-        g_scales = [keep.tile([P, N], U8, name="g_scales%d" % a, align_bytes=64) for a in range(PASSES)]
+        g_bf, g_scales = {}, {}
+        g_codes = [keep.tile([P, PASSES, P], U32, name="g_codes%d" % i, align_bytes=64) for i in range(2)]
         gaps, picked, means, banks = {}, {}, {}, {}
 
         def gather_x(i, a, cuts, fused):
-            gaps[i, a] = keep.tile([P, PASS], F32, name="gap%d%d" % (i, a))
+            gaps[i, a] = keep.tile([P, PASS], F32, name="gap%d%d" % (i, a), align_bytes=64)
             for q, (start, stop) in enumerate(zip(cuts[:-1], cuts[1:])):
                 two = keep.tile([P, stop - start], F32, name="two%d%d%d" % (i, a, q), align_bytes=64)
                 nc.scalar.activation(two[:], x_rows[i][:].indirect(entries(second, a, start, stop)), COPY)
@@ -113,7 +112,7 @@ def tile_list_moment_gaps_centred_columns_kernel(tc, xf, ra, gt, rb, old, offs, 
 
         def mean_g(i, a):
             sets = PASS // SET
-            total = keep.tile([P, sets], F32, name="total%d%d" % (i, a))
+            total = keep.tile([P, sets], F32, name="total%d%d" % (i, a), align_bytes=64)
             nc.vector.tensor_reduce(
                 total[:], picked[i, a][:].rearrange("p (c s) -> p c s", s=SET), mybir.AxisListType.X, ALU.add
             )
@@ -151,29 +150,32 @@ def tile_list_moment_gaps_centred_columns_kernel(tc, xf, ra, gt, rb, old, offs, 
             )
 
         def quantize_g(i, a):
-            cols = slice(i * P, (i + 1) * P)
             nc.vector.quantize_mx(
-                out=g_codes[a][:, cols].bitcast(E5M2X4), scales=g_scales[a][:, cols], in_=g_bf[i][:, a].rearrange("p c t -> p (c t)")
+                out=g_codes[i][:, a, :].bitcast(E5M2X4), scales=g_scales[i][:, a, :], in_=g_bf[i, a].rearrange("p c t -> p (c t)")
             )
 
         moments = [sums.tile([P, N], F32, name="moment%d" % i) for i in range(2)]
 
-        def multiply(i, a):
+        def multiply(i, a, n, start=False, stop=False):
             nc.tensor.matmul_mx(
-                out=moments[i][:],
+                out=moments[i][:, n * P : (n + 1) * P],
                 lhsT=u_codes[i][:, a, :].bitcast(E5M2X4),
                 lhsT_scale=u_scales[i][:, a, :],
-                rhs=g_codes[a][:].bitcast(E5M2X4),
-                rhs_scale=g_scales[a][:],
-                start=(a == 0),
-                stop=(a == PASSES - 1),
+                rhs=g_codes[n][:, a, :].bitcast(E5M2X4),
+                rhs_scale=g_scales[n][:, a, :],
+                start=start,
+                stop=stop,
             )
 
         def finish(i):
             w = keep.tile([P, N], F32, name="w%d" % i)
-            nc.scalar.copy(w[:], moments[i][:])
             cols = keep.tile([P, E], F32, name="cols%d" % i)
-            nc.vector.tensor_copy(cols[:], w[:].indirect(fourth[:]))
+            if i == 0:
+                nc.scalar.copy(w[:], moments[i][:])
+                nc.scalar.activation(cols[:], w[:].indirect(fourth[:]), COPY)
+            else:
+                nc.vector.tensor_copy(w[:], moments[i][:])
+                nc.vector.tensor_copy(cols[:], w[:].indirect(fourth[:]))
             y = keep.tile([P, E], F32, name="y%d" % i)
             nc.vector.scalar_tensor_tensor(y[:], cols[:], 0.04, old_t[:, i, :], ALU.mult, ALU.add)
             nc.sync.dma_start(out[i * P : (i + 1) * P, :], y[:])
@@ -190,24 +192,34 @@ def tile_list_moment_gaps_centred_columns_kernel(tc, xf, ra, gt, rb, old, offs, 
         for a in range(PASSES):
             gather_g(1, a)
             mean_g(1, a)
-            weigh(g_bf[0][:, a], banks["g", 0, a], rb_t, a)
             turn_g(1, a)
-        gather_x(1, 0, (0, 512), True)
-        gather_x(1, 1, (0, 384, 512), False)
-        g_bf.append(keep.tile([P, PASSES, P, PACK], BF16, name="two100", align_bytes=64))
+        g_bf[0, 0] = keep.tile([P, P, PACK], BF16, name="total10", align_bytes=64)[:]
+        weigh(g_bf[0, 0], banks["g", 0, 0], rb_t, 0)
+        gather_x(1, 0, (0, 256, 512), True)
+        gather_x(1, 1, (0, 256, 384, 512), False)
+        g_bf[0, 1] = keep.tile([P, P, PACK], BF16, name="two100", align_bytes=64)[:]
+        weigh(g_bf[0, 1], banks["g", 0, 1], rb_t, 1)
+        weigh_x(1, 0, (0, 512))
+        g_scales[0] = keep.tile([P, PASSES, P], U8, name="two101", align_bytes=64)
+        g_bf[1, 0] = keep.tile([P, P, PACK], BF16, name="gap10", align_bytes=64)[:]
         quantize_g(0, 0)
         quantize_g(0, 1)
-        weigh(g_bf[1][:, 0], banks["g", 1, 0], rb_t, 0)
-        weigh_x(1, 0, (0, 512))
-        quantize_g(1, 0)
-        weigh(g_bf[1][:, 1], banks["g", 1, 1], rb_t, 1)
+        weigh(g_bf[1, 0], banks["g", 1, 0], rb_t, 0)
         weigh_x(1, 1, (0, 384, 512))
-        quantize_g(1, 1)
-        for a in range(PASSES):
-            multiply(0, a)
+        multiply(0, 0, 0, start=True)
+        multiply(0, 1, 0)
+        g_bf[1, 1] = keep.tile([P, P, PACK], BF16, name="gap11", align_bytes=64)[:]
+        g_scales[1] = keep.tile([P, PASSES, P], U8, name="g_scales1", align_bytes=64)
+        weigh(g_bf[1, 1], banks["g", 1, 1], rb_t, 1)
+        quantize_g(1, 0)
         quantize_x(1, 0, 1)
-        multiply(1, 0)
+        quantize_g(1, 1)
         quantize_x(1, 1, 2)
-        multiply(1, 1)
+        multiply(0, 0, 1)
+        multiply(1, 0, 0, start=True)
+        multiply(1, 0, 1)
+        multiply(0, 1, 1, stop=True)
+        multiply(1, 1, 0)
+        multiply(1, 1, 1, stop=True)
         finish(0)
         finish(1)

from contextlib import ExitStack

import concourse.mybir as mybir
from concourse.masks import make_identity

K, J, N, T, E = 256, 1024, 256, 2048, 128
FLOPS = 2 * K * J * N

F32 = mybir.dt.float32
BF16 = mybir.dt.bfloat16
U32 = mybir.dt.uint32
U16 = mybir.dt.uint16
U8 = mybir.dt.uint8
E5M2X4 = mybir.dt.float8_e5m2_x4
ALU = mybir.AluOpType
COPY = mybir.ActivationFunctionType.Copy

P = 128
PACK = 4
PASS = P * PACK
PASSES = J // PASS
SET = 8
LIST_COLS = PASS // 16


def tile_list_moment_gaps_centred_columns_kernel(tc, xf, ra, gt, rb, old, offs, offs2, offs3, offs4, out):
    nc = tc.nc
    with ExitStack() as ctx:
        lists = ctx.enter_context(tc.tile_pool(name="lists", bufs=1))
        keep = ctx.enter_context(tc.tile_pool(name="keep", bufs=1))
        turn = ctx.enter_context(tc.psum_pool(name="turn", bufs=4))
        sums = ctx.enter_context(tc.psum_pool(name="sums", bufs=1))

        first = lists.tile([P, J // 16], U16, name="first")
        second = lists.tile([P, J // 16], U16, name="second")
        third = lists.tile([P, J // 16], U16, name="third")
        fourth = lists.tile([P, E // 16], U16, name="fourth")
        x_rows = [keep.tile([P, T], F32, name="x_rows%d" % i) for i in range(2)]
        g_rows = [keep.tile([P, T], F32, name="g_rows%d" % i) for i in range(2)]
        ra_t = keep.tile([P, PASSES, 8], F32, name="ra_t")
        rb_t = keep.tile([P, PASSES, 8], F32, name="rb_t")
        old_t = keep.tile([P, 2, E], F32, name="old_t")
        ident = keep.tile([P, P], F32, name="ident")

        nc.sync.dma_start(x_rows[0][:], xf[0:P, :])
        nc.sync.dma_start(second[:], offs2)
        nc.sync.dma_start(first[:], offs)
        nc.sync.dma_start(ra_t[:, :, 0:PACK], ra.rearrange("o (a p t) -> p (o a) t", p=P, t=PACK))
        nc.sync.dma_start(g_rows[0][:], gt[0:P, :])
        nc.sync.dma_start(third[:], offs3)
        nc.sync.dma_start(rb_t[:, :, 0:PACK], rb.rearrange("o (a p t) -> p (o a) t", p=P, t=PACK))
        nc.sync.dma_start(g_rows[1][:], gt[P : 2 * P, :])
        nc.sync.dma_start(x_rows[1][:], xf[P : 2 * P, :])
        nc.sync.dma_start(fourth[:], offs4)
        nc.sync.dma_start(old_t[:], old.rearrange("(i p) e -> p i e", p=P))
        warm = keep.tile([P, 8], F32, name="warm")
        nc.vector.memset(warm[:], 0.0)
        nc.scalar.activation(warm[:, 0:1], warm[:, 4:5], COPY)
        make_identity(nc, ident[:])

        def entries(lst, a, start=0, stop=PASS):
            return lst[:, a * LIST_COLS + start // 16 : a * LIST_COLS + stop // 16]

        ra_rows = [sums.tile([P, PACK, P], F32, name="ra_rows%d" % a) for a in range(PASSES)]
        for a in range(PASSES):
            for t in range(PACK):
                nc.tensor.transpose(ra_rows[a][:, t, :], ra_t[:, a, t : t + 1].to_broadcast([P, P]), ident[:])

        u_bf = [keep.tile([P, PASSES, P, PACK], BF16, name="u_bf%d" % i, align_bytes=64) for i in range(2)]
        u_codes = [keep.tile([P, PASSES, P], U32, name="u_codes%d" % i, align_bytes=64) for i in range(2)]
        u_scales = [keep.tile([P, PASSES, P], U8, name="u_scales%d" % i, align_bytes=64) for i in range(2)]
        g_bf, g_scales = {}, {}
        g_codes = [keep.tile([P, PASSES, P], U32, name="g_codes%d" % i, align_bytes=64) for i in range(2)]
        gaps, picked, means, banks = {}, {}, {}, {}

        def gather_x(i, a, cuts, fused):
            gaps[i, a] = keep.tile([P, PASS], F32, name="gap%d%d" % (i, a), align_bytes=64)
            for q, (start, stop) in enumerate(zip(cuts[:-1], cuts[1:])):
                two = keep.tile([P, stop - start], F32, name="two%d%d%d" % (i, a, q), align_bytes=64)
                nc.scalar.activation(two[:], x_rows[i][:].indirect(entries(second, a, start, stop)), COPY)
                if fused:
                    nc.vector.tensor_tensor(
                        gaps[i, a][:, start:stop], x_rows[i][:].indirect(entries(first, a, start, stop)), two[:], ALU.subtract
                    )
                else:
                    one = keep.tile([P, stop - start], F32, name="one%d%d%d" % (i, a, q))
                    nc.scalar.activation(one[:], x_rows[i][:].indirect(entries(first, a, start, stop)), COPY)
                    nc.gpsimd.tensor_tensor(gaps[i, a][:, start:stop], one[:], two[:], ALU.subtract)

        def weigh_x(i, a, cuts):
            rounded = keep.tile([P, P, PACK], BF16, name="rounded%d%d" % (i, a))
            for start, stop in zip(cuts[:-1], cuts[1:]):
                ps = slice(start // PACK, stop // PACK)
                nc.vector.tensor_tensor(
                    rounded[:, ps, :],
                    ra_rows[a][:, :, ps].rearrange("k t p -> k p t"),
                    gaps[i, a][:, start:stop].rearrange("k (p t) -> k p t", t=PACK),
                    ALU.mult,
                )
            words = rounded[:].rearrange("k p t -> k (p t)").bitcast(F32)
            bank = turn.tile([P, 2, P], F32, name="bank")
            for u in range(2):
                nc.tensor.transpose(bank[:, u, :], words[:, u::2], ident[:])
            nc.scalar.copy(
                u_bf[i][:, a].rearrange("p c t -> p (c t)").bitcast(F32).rearrange("p (c u) -> p c u", u=2),
                bank[:].rearrange("p u c -> p c u"),
            )

        def gather_g(i, a):
            picked[i, a] = keep.tile([P, PASS], F32, name="picked%d%d" % (i, a))
            nc.scalar.activation(picked[i, a][:], g_rows[i][:].indirect(entries(third, a)), COPY)

        def mean_g(i, a):
            sets = PASS // SET
            total = keep.tile([P, sets], F32, name="total%d%d" % (i, a), align_bytes=64)
            nc.vector.tensor_reduce(
                total[:], picked[i, a][:].rearrange("p (c s) -> p c s", s=SET), mybir.AxisListType.X, ALU.add
            )
            means[i, a] = keep.tile([P, sets, 2], F32, name="mean%d%d" % (i, a))
            nc.gpsimd.tensor_scalar(
                means[i, a][:], total[:].unsqueeze(2).to_broadcast([P, sets, 2]), -1.0 / SET, 0.0, ALU.mult, ALU.add
            )

        def turn_x(i, a):
            bank = turn.tile([P, PACK, P], F32, name="bank")
            banks["x", i, a] = bank
            for t in range(PACK):
                nc.tensor.transpose(bank[:, t, :], gaps[i, a][:, t::PACK], ident[:])

        def turn_g(i, a):
            bank = turn.tile([P, PACK, P], F32, name="bank")
            banks["g", i, a] = bank
            for t in range(PACK):
                nc.tensor.matmul(bank[:, t, :], picked[i, a][:, t::PACK], ident[:], start=(t == 0), stop=False, is_transpose=True)
            for t in range(PACK):
                nc.tensor.matmul(
                    bank[:, t, :], means[i, a][:].rearrange("p c e -> p (c e)"), ident[:], start=False, stop=(t == PACK - 1), is_transpose=True
                )

        def weigh(dst, bank, weights, a):
            nc.vector.tensor_tensor(
                dst, bank[:].rearrange("p t c -> p c t"), weights[:, a : a + 1, 0:PACK].to_broadcast([P, P, PACK]), ALU.mult
            )

        def quantize_x(i, a0, a1):
            nc.vector.quantize_mx(
                out=u_codes[i][:, a0:a1, :].rearrange("p a c -> p (a c)").bitcast(E5M2X4),
                scales=u_scales[i][:, a0:a1, :].rearrange("p a c -> p (a c)"),
                in_=u_bf[i][:, a0:a1].rearrange("p a c t -> p (a c t)"),
            )

        def quantize_g(i, a):
            nc.vector.quantize_mx(
                out=g_codes[i][:, a, :].bitcast(E5M2X4), scales=g_scales[i][:, a, :], in_=g_bf[i, a].rearrange("p c t -> p (c t)")
            )

        moments = [sums.tile([P, N], F32, name="moment%d" % i) for i in range(2)]

        def multiply(i, a, n, start=False, stop=False):
            nc.tensor.matmul_mx(
                out=moments[i][:, n * P : (n + 1) * P],
                lhsT=u_codes[i][:, a, :].bitcast(E5M2X4),
                lhsT_scale=u_scales[i][:, a, :],
                rhs=g_codes[n][:, a, :].bitcast(E5M2X4),
                rhs_scale=g_scales[n][:, a, :],
                start=start,
                stop=stop,
            )

        def finish(i):
            w = keep.tile([P, N], F32, name="w%d" % i)
            cols = keep.tile([P, E], F32, name="cols%d" % i)
            if i == 0:
                nc.scalar.copy(w[:], moments[i][:])
                nc.scalar.activation(cols[:], w[:].indirect(fourth[:]), COPY)
            else:
                nc.vector.tensor_copy(w[:], moments[i][:])
                nc.vector.tensor_copy(cols[:], w[:].indirect(fourth[:]))
            y = keep.tile([P, E], F32, name="y%d" % i)
            nc.vector.scalar_tensor_tensor(y[:], cols[:], 0.04, old_t[:, i, :], ALU.mult, ALU.add)
            nc.sync.dma_start(out[i * P : (i + 1) * P, :], y[:])

        for a in range(PASSES):
            gather_x(0, a, (0, 256, 512), True)
            turn_x(0, a)
        for a in range(PASSES):
            gather_g(0, a)
            weigh(u_bf[0][:, a], banks["x", 0, a], ra_t, a)
            mean_g(0, a)
            turn_g(0, a)
        quantize_x(0, 0, 2)
        for a in range(PASSES):
            gather_g(1, a)
            mean_g(1, a)
            turn_g(1, a)
        g_bf[0, 0] = keep.tile([P, P, PACK], BF16, name="total10", align_bytes=64)[:]
        weigh(g_bf[0, 0], banks["g", 0, 0], rb_t, 0)
        gather_x(1, 0, (0, 256, 512), True)
        gather_x(1, 1, (0, 256, 384, 512), False)
        g_bf[0, 1] = keep.tile([P, P, PACK], BF16, name="two100", align_bytes=64)[:]
        weigh(g_bf[0, 1], banks["g", 0, 1], rb_t, 1)
        weigh_x(1, 0, (0, 512))
        g_scales[0] = keep.tile([P, PASSES, P], U8, name="two101", align_bytes=64)
        g_bf[1, 0] = keep.tile([P, P, PACK], BF16, name="gap10", align_bytes=64)[:]
        quantize_g(0, 0)
        quantize_g(0, 1)
        weigh(g_bf[1, 0], banks["g", 1, 0], rb_t, 0)
        weigh_x(1, 1, (0, 384, 512))
        multiply(0, 0, 0, start=True)
        multiply(0, 1, 0)
        g_bf[1, 1] = keep.tile([P, P, PACK], BF16, name="gap11", align_bytes=64)[:]
        g_scales[1] = keep.tile([P, PASSES, P], U8, name="g_scales1", align_bytes=64)
        weigh(g_bf[1, 1], banks["g", 1, 1], rb_t, 1)
        quantize_g(1, 0)
        quantize_x(1, 0, 1)
        quantize_g(1, 1)
        quantize_x(1, 1, 2)
        multiply(0, 0, 1)
        multiply(1, 0, 0, start=True)
        multiply(1, 0, 1)
        multiply(0, 1, 1, stop=True)
        multiply(1, 1, 0)
        multiply(1, 1, 1, stop=True)
        finish(0)
        finish(1)
